import numpy as np
import ml_dtypes


def mxq(x, axis, fmt="e4m3"):
    dtype, down = {"e4m3": (ml_dtypes.float8_e4m3fn, 7), "e5m2": (ml_dtypes.float8_e5m2, 14)}[fmt]
    v = np.moveaxis(np.asarray(x, np.float32).astype(ml_dtypes.bfloat16).astype(np.float64), axis, -1)
    blocks = v.reshape(v.shape[:-1] + (-1, 32))
    amax = np.abs(blocks).max(-1, keepdims=True)
    byte = np.maximum(np.where(amax > 0, np.frexp(amax)[1] - 1 + 127, 0) - down, 1)
    scale = np.exp2(byte - 127.0)
    codes = (blocks / scale).astype(np.float32).astype(dtype).astype(np.float64)
    return np.moveaxis((codes * scale).reshape(v.shape), -1, axis)


WIDE = False


def mx_kscale(k):
    if not WIDE:
        return np.ones(k)
    levels = np.array([10, -10, 5, -5, 0])
    if k % 512:
        return np.exp2(np.random.permutation(np.resize(levels, k // 32))).repeat(32)
    a = np.empty((k // 512, 16))
    for p in range(k // 512):
        a[p, :8] = np.random.permutation(np.resize(levels, 8))
        for g in range(8):
            far = levels[np.abs(levels - a[p, g]) >= 10]
            a[p, g + 8] = far[np.random.randint(len(far))]
    return np.exp2(a.ravel()).repeat(32)


def f64(x):
    return np.asarray(x).astype(np.float64)


def striped(idx):
    return np.tile(idx.reshape(-1, 16).T, (8, 1)).astype(np.uint16)


def unstriped(offs):
    return offs[:16].T.reshape(-1).astype(np.int64)


def gelu(v):
    return 0.5 * v * (1.0 + np.tanh(np.sqrt(2.0 / np.pi) * (v + 0.044715 * v**3)))


K, T, S, V, H, N = 512, 1024, 512, 256, 512, 256


def setup_inputs():
    n = np.random.standard_normal
    s = mx_kscale(K)[:, None]
    u = mx_kscale(H)
    return {
        "xT": (n((K, T)) * s).astype(np.float32),
        "w1": (n((K, H)) / np.sqrt(2 * K) / s * u).astype(np.float32),
        "w2": (n((K, H)) / np.sqrt(2 * K) / s * u).astype(np.float32),
        "w3": (n((H, N)) / np.sqrt(H) / u[:, None]).astype(np.float32),
        "offs": striped(np.random.permutation(T)[:S]),
        "cen": striped(np.random.permutation(S)[:V]),
        "pos1": striped(np.random.permutation(S)[:V]),
        "pos2": striped(np.random.permutation(S)[:V]),
        "pos3": striped(np.random.permutation(S)[:V]),
        "pos4": striped(np.random.permutation(S)[:V]),
    }


def reference(xT, w1, w2, w3, offs, cen, pos1, pos2, pos3, pos4):
    xq = mxq(f64(xT)[:, unstriped(offs)], 0, "e4m3")
    y = mxq(f64(w1), 0, "e4m3").T @ xq
    yc = y[:, unstriped(cen)]
    e = mxq(f64(w2), 0, "e4m3").T @ xq
    z = np.maximum(np.maximum(np.maximum(gelu(yc + e[:, unstriped(pos1)]), gelu(yc + e[:, unstriped(pos2)])), gelu(yc + e[:, unstriped(pos3)])), gelu(yc + e[:, unstriped(pos4)]))
    return mxq(f64(w3), 0, "e4m3").T @ mxq(z, 0, "e4m3")

@@ -1,0 +1,199 @@
+from contextlib import ExitStack
+
+import concourse.mybir as mybir
+
+K, T, S, V, H, N = 512, 1024, 512, 256, 512, 256
+D = 4
+P = 128
+PACK = 4
+FLOPS = 2 * (2 * K * H * S + H * N * V)
+
+F32 = mybir.dt.float32
+BF16 = mybir.dt.bfloat16
+U32 = mybir.dt.uint32
+U16 = mybir.dt.uint16
+U8 = mybir.dt.uint8
+FP8X4 = mybir.dt.float8_e4m3fn_x4
+ADD = mybir.AluOpType.add
+MAX = mybir.AluOpType.max
+GELU = mybir.ActivationFunctionType.Gelu_apprx_tanh
+
+
+def tile_picked_edgecv_gelu_e_kernel(tc, xT, w1, w2, w3, offs, cen, pos1, pos2, pos3, pos4, out):
+    nc = tc.nc
+    with ExitStack() as ctx:
+        keep = ctx.enter_context(tc.tile_pool(name="keep", bufs=1))
+        psum = ctx.enter_context(tc.psum_pool(name="psum", bufs=8))
+
+        def load_list(src, name):
+            tile = keep.tile([P, src.shape[1]], U16, name=name)
+            nc.sync.dma_start(tile[:], src)
+            return tile
+
+        def mx_tiles(width, name):
+            codes = keep.tile([P, width], U32, name=name + "_codes", align_bytes=64)
+            scales = keep.tile([P, width], U8, name=name + "_scales", align_bytes=64)
+            return codes, scales
+
+        def quantize(mx, woven, c0, c1):
+            nc.vector.quantize_mx(
+                out=mx[0][:, c0:c1].bitcast(FP8X4), scales=mx[1][:, c0:c1], in_=woven[:, PACK * c0 : PACK * c1]
+            )
+
+        def product(acc, lhs, l0, l1, rhs, r0, r1):
+            nc.tensor.matmul_mx(
+                out=acc,
+                lhsT=lhs[0][:, l0:l1].bitcast(FP8X4),
+                lhsT_scale=lhs[1][:, l0:l1],
+                rhs=rhs[0][:, r0:r1].bitcast(FP8X4),
+                rhs_scale=rhs[1][:, r0:r1],
+                start=True,
+                stop=True,
+            )
+
+        offs_sb = load_list(offs, "offs_sb")
+        x_rows = xT.rearrange("(p j) t -> j p t", j=PACK)
+        x_plane = []
+        for j in range(PACK):
+            tile = keep.tile([P, T], F32, name="x_plane%d" % j)
+            nc.sync.dma_start(tile[:], x_rows[j])
+            x_plane.append(tile)
+        w1_raw = keep.tile([P, PACK, H], F32, name="w1_raw")
+        nc.sync.dma_start(w1_raw[:], w1.rearrange("(p j) i -> p j i", j=PACK))
+        cen_sb = load_list(cen, "cen_sb")
+        w2_raw = keep.tile([P, PACK, H], F32, name="w2_raw")
+        nc.sync.dma_start(w2_raw[:], w2.rearrange("(p j) i -> p j i", j=PACK))
+        pos_sb = [load_list(src, "pos%d_sb" % d) for d, src in enumerate((pos1, pos2, pos3, pos4))]
+        w3_raw = keep.tile([P, PACK, N], F32, name="w3_raw")
+        w3_rows = w3.rearrange("(q t b) m -> b q t m", t=PACK, b=PACK)
+        for b in range(PACK):
+            nc.sync.dma_start(w3_raw[b:P:PACK, :, :], w3_rows[b])
+
+        warm = keep.tile([P, 8], F32, name="warm")
+        warm_out = keep.tile([P, 8], F32, name="warm_out")
+        nc.gpsimd.memset(warm[:], 0.0)
+        nc.scalar.activation(warm_out[:], warm[:], GELU)
+
+        x_woven = keep.tile([P, S * PACK], BF16, name="x_woven", align_bytes=64)
+        x_slots = x_woven[:].rearrange("p (n j) -> p n j", j=PACK)
+        x_mx = mx_tiles(S, "x")
+        pair01 = keep.tile([P, 2, S], BF16, name="pair01")
+        for j in range(2):
+            nc.vector.tensor_copy(pair01[:, j, :], x_plane[j][:].indirect(offs_sb[:]))
+        nc.scalar.copy(x_slots[:, :, 0:2], pair01[:].rearrange("p j n -> p n j"))
+        half = S // 2
+        pair23 = [keep.tile([P, 2, half], BF16, name="pair23_%d" % h) for h in range(2)]
+        for j in range(2):
+            for h in range(2):
+                nc.vector.tensor_copy(
+                    pair23[h][:, j, :], x_plane[2 + j][:].indirect(offs_sb[:, h * half // 16 : (h + 1) * half // 16])
+                )
+        for h in range(2):
+            nc.vector.tensor_copy(x_slots[:, h * half : (h + 1) * half, 2:4], pair23[h][:].rearrange("p j n -> p n j"))
+        for h in range(2):
+            quantize(x_mx, x_woven, h * half, (h + 1) * half)
+
+        def weave_w(copy, raw, t, name):
+            woven = keep.tile([P, P * PACK], BF16, name=name, align_bytes=64)
+            copy(
+                woven[:].rearrange("p (q b j) -> p q j b", b=PACK, j=PACK),
+                raw[:].rearrange("p j (q t b) -> p t q j b", t=PACK, b=PACK)[:, t],
+            )
+            return woven
+
+        def quantize_w(woven, name):
+            mx = mx_tiles(P, name)
+            quantize(mx, woven, 0, P)
+            return mx
+
+        def multiply(w_mx):
+            acc = psum.tile([P, S], F32, name="acc")
+            product(acc[:], w_mx, 0, P, x_mx, 0, S)
+            return acc
+
+        def evacuate(acc, name):
+            rows = keep.tile([P, S], F32, name=name)
+            nc.scalar.copy(rows[:], acc[:])
+            return rows
+
+        centre = keep.tile([P, PACK, V], F32, name="centre")
+        edge = [keep.tile([P, PACK, V], F32, name="edge%d" % d) for d in range(D)]
+
+        def fetch_centre(y, t):
+            nc.vector.tensor_copy(centre[:, t, :], y[:].indirect(cen_sb[:]))
+
+        def fetch_edge(e, t, d, v0, v1):
+            nc.vector.tensor_tensor(
+                edge[d][:, t, v0:v1], e[:].indirect(pos_sb[d][:, v0 // 16 : v1 // 16]), centre[:, t, v0:v1], ADD
+            )
+
+        w1_woven = [weave_w(nc.scalar.copy, w1_raw, 0, "w1_woven0")]
+        y_acc = [multiply(quantize_w(w1_woven[0], "w1_0"))]
+        for t in range(1, PACK):
+            w1_woven.append(weave_w(nc.vector.tensor_copy, w1_raw, t, "w1_woven%d" % t))
+        for t in range(1, PACK):
+            y_acc.append(multiply(quantize_w(w1_woven[t], "w1_%d" % t)))
+        y = [evacuate(y_acc[0], "y0")]
+        fetch_centre(y[0], 0)
+        w2_woven = weave_w(nc.vector.tensor_copy, w2_raw, 0, "w2_woven0")
+        y.append(evacuate(y_acc[1], "y1"))
+        fetch_centre(y[1], 1)
+        e_acc = multiply(quantize_w(w2_woven, "w2_0"))
+        for t in range(2, PACK):
+            y.append(evacuate(y_acc[t], "y%d" % t))
+            fetch_centre(y[t], t)
+        e = []
+        for t in range(PACK):
+            if t + 1 < PACK:
+                w2_woven = weave_w(nc.scalar.copy, w2_raw, t + 1, "w2_woven%d" % (t + 1))
+            e.append(evacuate(e_acc, "e%d" % t))
+            if t + 1 < PACK:
+                e_acc = multiply(quantize_w(w2_woven, "w2_%d" % (t + 1)))
+            fetch_edge(e[t], t, 0, 0, V)
+            fetch_edge(e[t], t, 1, 0, V)
+
+        w3_woven = keep.tile([P, N * PACK], BF16, name="w3_woven", align_bytes=64)
+        nc.scalar.copy(
+            w3_woven[:].rearrange("p (c i t) -> p c t i", i=4, t=PACK),
+            w3_raw[:].rearrange("p t (c i) -> p c t i", i=4),
+        )
+
+        act = [keep.tile([P, V * PACK], BF16, name="act%d" % d) for d in range(D)]
+
+        def gelu(d, v0, v1):
+            nc.scalar.activation(
+                act[d][:, PACK * v0 : PACK * v1].rearrange("p (c i t) -> p c t i", i=4, t=PACK),
+                edge[d][:, :, v0:v1].rearrange("p t (c i) -> p c t i", i=4),
+                GELU,
+            )
+
+        gelu(0, 0, V)
+        gelu(1, 0, V)
+        for t in range(PACK):
+            fetch_edge(e[t], t, 2, 0, V)
+        w3_mx = mx_tiles(N, "w3")
+        quantize(w3_mx, w3_woven, 0, N)
+        gelu(2, 0, V)
+        max01 = keep.tile([P, V * PACK], BF16, name="max01")
+        max012 = keep.tile([P, V * PACK], BF16, name="max012")
+        z_woven = keep.tile([P, V * PACK], BF16, name="z_woven", align_bytes=64)
+        z_mx = mx_tiles(V, "z")
+        nc.vector.tensor_tensor(max01[:], act[0][:], act[1][:], MAX)
+        chunks = [(0, V // 2), (V // 2, V)]
+        for c, (v0, v1) in enumerate(chunks):
+            for t in range(PACK):
+                fetch_edge(e[t], t, 3, v0, v1)
+            if c == 0:
+                nc.vector.tensor_tensor(max012[:], max01[:], act[2][:], MAX)
+            gelu(3, v0, v1)
+        out_rows = out.rearrange("(a p) v -> p a v", p=P)
+        for c, (v0, v1) in enumerate(chunks):
+            cols = slice(PACK * v0, PACK * v1)
+            nc.vector.tensor_tensor(z_woven[:, cols], max012[:, cols], act[3][:, cols], MAX)
+            quantize(z_mx, z_woven, v0, v1)
+            acc = psum.tile([P, 2, v1 - v0], F32, name="acc")
+            for a in range(2):
+                product(acc[:, a, :], w3_mx, a * P, (a + 1) * P, z_mx, v0, v1)
+            result = keep.tile([P, 2, v1 - v0], F32, name="result%d" % c)
+            nc.scalar.copy(result[:], acc[:])
+            nc.sync.dma_start(out_rows[:, :, v0:v1], result[:])

@@ -16,6 +16,7 @@ U8 = mybir.dt.uint8
 FP8X4 = mybir.dt.float8_e4m3fn_x4
 ADD = mybir.AluOpType.add
 MAX = mybir.AluOpType.max
+COPY = mybir.ActivationFunctionType.Copy
 GELU = mybir.ActivationFunctionType.Gelu_apprx_tanh
 
 
@@ -31,7 +32,7 @@ def tile_picked_edgecv_gelu_e_kernel(tc, xT, w1, w2, w3, offs, cen, pos1, pos2, 
             return tile
 
         def mx_tiles(width, name):
-            codes = keep.tile([P, width], U32, name=name + "_codes", align_bytes=64)
+            codes = keep.tile([P, width], U32, name=name + "_codes", tag=name + "_codes", align_bytes=64)
             scales = keep.tile([P, width], U8, name=name + "_scales", align_bytes=64)
             return codes, scales
 
@@ -74,29 +75,35 @@ def tile_picked_edgecv_gelu_e_kernel(tc, xT, w1, w2, w3, offs, cen, pos1, pos2, 
         nc.gpsimd.memset(warm[:], 0.0)
         nc.scalar.activation(warm_out[:], warm[:], GELU)
 
-        x_woven = keep.tile([P, S * PACK], BF16, name="x_woven", align_bytes=64)
-        x_slots = x_woven[:].rearrange("p (n j) -> p n j", j=PACK)
-        x_mx = mx_tiles(S, "x")
-        pair01 = keep.tile([P, 2, S], BF16, name="pair01")
-        for j in range(2):
-            nc.vector.tensor_copy(pair01[:, j, :], x_plane[j][:].indirect(offs_sb[:]))
-        nc.scalar.copy(x_slots[:, :, 0:2], pair01[:].rearrange("p j n -> p n j"))
         half = S // 2
-        pair23 = [keep.tile([P, 2, half], BF16, name="pair23_%d" % h) for h in range(2)]
+        x_woven = [keep.tile([P, half * PACK], BF16, name="x_woven%d" % h, tag="x_woven%d" % h, align_bytes=64) for h in range(2)]
+        x_slots = [tile[:].rearrange("p (n j) -> p n j", j=PACK) for tile in x_woven]
+        x_mx = mx_tiles(S, "x")
+        for j in range(2):
+            rounded = keep.tile([P, T], BF16, name="x_rounded%d" % j)
+            nc.vector.tensor_copy(rounded[:], x_plane[j][:])
+            for h in range(2):
+                nc.scalar.activation(
+                    x_slots[h][:, :, j], rounded[:].indirect(offs_sb[:, h * half // 16 : (h + 1) * half // 16]), COPY
+                )
+        pair23 = [keep.tile([P, 2, half], BF16, name="pair23_%d" % h, tag="pair23_%d" % h, align_bytes=64) for h in range(2)]
         for j in range(2):
             for h in range(2):
                 nc.vector.tensor_copy(
                     pair23[h][:, j, :], x_plane[2 + j][:].indirect(offs_sb[:, h * half // 16 : (h + 1) * half // 16])
                 )
+        for h, copy in enumerate((nc.scalar.copy, nc.vector.tensor_copy)):
+            copy(x_slots[h][:, :, 2:4], pair23[h][:].rearrange("p j n -> p n j"))
         for h in range(2):
-            nc.vector.tensor_copy(x_slots[:, h * half : (h + 1) * half, 2:4], pair23[h][:].rearrange("p j n -> p n j"))
-        for h in range(2):
-            quantize(x_mx, x_woven, h * half, (h + 1) * half)
+            nc.vector.quantize_mx(
+                out=x_mx[0][:, h * half : (h + 1) * half].bitcast(FP8X4),
+                scales=x_mx[1][:, h * half : (h + 1) * half],
+                in_=x_woven[h][:],
+            )
 
-        def weave_w(copy, raw, t, name):
-            woven = keep.tile([P, P * PACK], BF16, name=name, align_bytes=64)
+        def weave_w(copy, raw, t, woven):
             copy(
-                woven[:].rearrange("p (q b j) -> p q j b", b=PACK, j=PACK),
+                woven.rearrange("p (q b j) -> p q j b", b=PACK, j=PACK),
                 raw[:].rearrange("p j (q t b) -> p t q j b", t=PACK, b=PACK)[:, t],
             )
             return woven
@@ -116,80 +123,114 @@ def tile_picked_edgecv_gelu_e_kernel(tc, xT, w1, w2, w3, offs, cen, pos1, pos2, 
             nc.scalar.copy(rows[:], acc[:])
             return rows
 
-        centre = keep.tile([P, PACK, V], F32, name="centre")
-        edge = [keep.tile([P, PACK, V], F32, name="edge%d" % d) for d in range(D)]
+        def reuse(tag, shape, dtype, name):
+            return keep.tile(shape, dtype, name=name, tag=tag, align_bytes=64)
+
+        centre = [keep.tile([P, V], F32, name="centre%d" % t) for t in range(PACK)]
+        act = [keep.tile([P, D, V], BF16, name="act%d" % t) for t in range(PACK)]
+        pairmax = [keep.tile([P, 2, V], BF16, name="pairmax%d" % t) for t in range(PACK)]
+        z_early = keep.tile([P, PACK - 1, V], BF16, name="z_early")
+        z_woven = keep.tile([P, V * PACK], BF16, name="z_woven", align_bytes=64)
+        z_slots = z_woven[:].rearrange("p (v t) -> p v t", t=PACK)
+        z_mx = mx_tiles(V, "z")
 
         def fetch_centre(y, t):
-            nc.vector.tensor_copy(centre[:, t, :], y[:].indirect(cen_sb[:]))
+            nc.vector.tensor_copy(centre[t][:], y[:].indirect(cen_sb[:]))
 
-        def fetch_edge(e, t, d, v0, v1):
+        def fetch_edge(dst, e, t, d, v0, v1):
             nc.vector.tensor_tensor(
-                edge[d][:, t, v0:v1], e[:].indirect(pos_sb[d][:, v0 // 16 : v1 // 16]), centre[:, t, v0:v1], ADD
+                dst[:, v0:v1], e[:].indirect(pos_sb[d][:, v0 // 16 : v1 // 16]), centre[t][:, v0:v1], ADD
             )
 
-        w1_woven = [weave_w(nc.scalar.copy, w1_raw, 0, "w1_woven0")]
-        y_acc = [multiply(quantize_w(w1_woven[0], "w1_0"))]
-        for t in range(1, PACK):
-            w1_woven.append(weave_w(nc.vector.tensor_copy, w1_raw, t, "w1_woven%d" % t))
-        for t in range(1, PACK):
-            y_acc.append(multiply(quantize_w(w1_woven[t], "w1_%d" % t)))
-        y = [evacuate(y_acc[0], "y0")]
-        fetch_centre(y[0], 0)
-        w2_woven = weave_w(nc.vector.tensor_copy, w2_raw, 0, "w2_woven0")
-        y.append(evacuate(y_acc[1], "y1"))
-        fetch_centre(y[1], 1)
-        e_acc = multiply(quantize_w(w2_woven, "w2_0"))
-        for t in range(2, PACK):
-            y.append(evacuate(y_acc[t], "y%d" % t))
-            fetch_centre(y[t], t)
-        e = []
-        for t in range(PACK):
-            if t + 1 < PACK:
-                w2_woven = weave_w(nc.scalar.copy, w2_raw, t + 1, "w2_woven%d" % (t + 1))
-            e.append(evacuate(e_acc, "e%d" % t))
-            if t + 1 < PACK:
-                e_acc = multiply(quantize_w(w2_woven, "w2_%d" % (t + 1)))
-            fetch_edge(e[t], t, 0, 0, V)
-            fetch_edge(e[t], t, 1, 0, V)
+        def largest(t):
+            nc.vector.tensor_tensor(pairmax[t][:], act[t][:, 0:2, :], act[t][:, 2:4, :], MAX)
+            nc.vector.tensor_tensor(z_early[:, t, :], pairmax[t][:, 0, :], pairmax[t][:, 1, :], MAX)
 
-        w3_woven = keep.tile([P, N * PACK], BF16, name="w3_woven", align_bytes=64)
+        last = PACK - 1
+        tile = reuse("pair23_0", [P, P * PACK], BF16, "w1_woven0")
+        w1_first = quantize_w(weave_w(nc.scalar.copy, w1_raw, 0, tile[:]), "w1_0")
+        y0 = keep.tile([P, S], F32, name="y0")
+        for h in range(2):
+            acc = psum.tile([P, half], F32, name="acc")
+            product(acc[:], w1_first, 0, P, x_mx, h * half, (h + 1) * half)
+            nc.scalar.copy(y0[:, h * half : (h + 1) * half], acc[:])
+        tile = reuse("pair23_1", [P, P * PACK], BF16, "w1_woven1")
+        y_acc = [None, multiply(quantize_w(weave_w(nc.scalar.copy, w1_raw, 1, tile[:]), "w1_1"))]
+        tile = reuse("pair23_0", [P, 2 * P * PACK], BF16, "w1_woven23")
+        nc.vector.tensor_copy(
+            tile[:].rearrange("p (t q b j) -> p t q j b", t=2, b=PACK, j=PACK),
+            w1_raw[:].rearrange("p j (q t b) -> p t q j b", t=PACK, b=PACK)[:, 2:4],
+        )
+        w1_late = mx_tiles(2 * P, "w1_3")
+        quantize(w1_late, tile, 0, 2 * P)
+        for t in range(2):
+            acc = psum.tile([P, S], F32, name="acc")
+            product(acc[:], w1_late, t * P, (t + 1) * P, x_mx, 0, S)
+            y_acc.append(acc)
+
+        def w2_stage(copy, t, tag):
+            tile = reuse(tag, [P, P * PACK], BF16, "w2_woven%d" % t)
+            return weave_w(copy, w2_raw, t, tile[:])
+
+        w2_woven = w2_stage(nc.vector.tensor_copy, 0, "pair23_0")
+        fetch_centre(y0, 0)
+        e_acc = [multiply(quantize_w(w2_woven, "w2_0"))]
+        fetch_centre(evacuate(y_acc[1], "y1"), 1)
+        fetch_centre(evacuate(y_acc[2], "y2"), 2)
+        fetch_centre(evacuate(y_acc[last], "y3"), last)
+        w2_woven = w2_stage(nc.scalar.copy, 1, "w1_3_codes")
+        e_acc.append(multiply(quantize_w(w2_woven, "w2_1")))
+        e = [evacuate(e_acc[0], "e0")]
+        w2_woven = w2_stage(nc.scalar.copy, 2, "w2_0_codes")
+        edge0 = reuse("edge_even", [P, D, V], F32, "edge0")
+        for d in range(D):
+            fetch_edge(edge0[:, d, :], e[0], 0, d, 0, V)
+        e_acc.append(multiply(quantize_w(w2_woven, "w2_2")))
+        e.append(evacuate(e_acc[1], "e1"))
+        w2_woven = w2_stage(nc.scalar.copy, 3, "w2_1_codes")
+        e_acc.append(multiply(quantize_w(w2_woven, "w2_3")))
+        edge1 = reuse("edge_odd", [P, D, V], F32, "edge1")
+        for d in range(D):
+            fetch_edge(edge1[:, d, :], e[1], 1, d, 0, V)
+        e.append(evacuate(e_acc[2], "e2"))
+        nc.scalar.activation(act[0][:], edge0[:], GELU)
+        e.append(evacuate(e_acc[3], "e3"))
+        largest(0)
+
+        w3_woven = reuse("w2_2_codes", [P, N * PACK], BF16, "w3_woven")
         nc.scalar.copy(
             w3_woven[:].rearrange("p (c i t) -> p c t i", i=4, t=PACK),
             w3_raw[:].rearrange("p t (c i) -> p c t i", i=4),
         )
-
-        act = [keep.tile([P, V * PACK], BF16, name="act%d" % d) for d in range(D)]
-
-        def gelu(d, v0, v1):
-            nc.scalar.activation(
-                act[d][:, PACK * v0 : PACK * v1].rearrange("p (c i t) -> p c t i", i=4, t=PACK),
-                edge[d][:, :, v0:v1].rearrange("p t (c i) -> p c t i", i=4),
-                GELU,
-            )
-
-        gelu(0, 0, V)
-        gelu(1, 0, V)
-        for t in range(PACK):
-            fetch_edge(e[t], t, 2, 0, V)
+        edge2 = reuse("edge_even", [P, D, V], F32, "edge2")
+        nc.scalar.activation(act[1][:], edge1[:], GELU)
+        for d in range(D):
+            fetch_edge(edge2[:, d, :], e[2], 2, d, 0, V)
+            if d % 2 == 1:
+                nc.scalar.activation(act[2][:, d - 1 : d + 1, :], edge2[:, d - 1 : d + 1, :], GELU)
         w3_mx = mx_tiles(N, "w3")
         quantize(w3_mx, w3_woven, 0, N)
-        gelu(2, 0, V)
-        max01 = keep.tile([P, V * PACK], BF16, name="max01")
-        max012 = keep.tile([P, V * PACK], BF16, name="max012")
-        z_woven = keep.tile([P, V * PACK], BF16, name="z_woven", align_bytes=64)
-        z_mx = mx_tiles(V, "z")
-        nc.vector.tensor_tensor(max01[:], act[0][:], act[1][:], MAX)
+        largest(1)
+        edge3a = reuse("edge_odd", [P, V], F32, "edge3a")
+        fetch_edge(edge3a[:], e[3], last, 0, 0, V)
+        largest(2)
+        nc.scalar.copy(z_slots[:, :, 0:last], z_early[:].rearrange("p t v -> p v t"))
+        nc.scalar.activation(act[last][:, 0, :], edge3a[:], GELU)
+        edge3b = reuse("edge_even", [P, D - 1, V], F32, "edge3b")
+        for d in (1, 2):
+            fetch_edge(edge3b[:, d - 1, :], e[3], last, d, 0, V)
+            nc.scalar.activation(act[last][:, d, :], edge3b[:, d - 1, :], GELU)
         chunks = [(0, V // 2), (V // 2, V)]
         for c, (v0, v1) in enumerate(chunks):
-            for t in range(PACK):
-                fetch_edge(e[t], t, 3, v0, v1)
+            fetch_edge(edge3b[:, 2, :], e[3], last, 3, v0, v1)
+            nc.scalar.activation(act[last][:, 3, v0:v1], edge3b[:, 2, v0:v1], GELU)
             if c == 0:
-                nc.vector.tensor_tensor(max012[:], max01[:], act[2][:], MAX)
-            gelu(3, v0, v1)
+                nc.vector.tensor_tensor(pairmax[last][:, 0, :], act[last][:, 0, :], act[last][:, 1, :], MAX)
+        nc.vector.tensor_tensor(pairmax[last][:, 1, :], pairmax[last][:, 0, :], act[last][:, 2, :], MAX)
         out_rows = out.rearrange("(a p) v -> p a v", p=P)
+        for v0, v1 in chunks:
+            nc.vector.tensor_tensor(z_slots[:, v0:v1, last], pairmax[last][:, 1, v0:v1], act[last][:, 3, v0:v1], MAX)
         for c, (v0, v1) in enumerate(chunks):
-            cols = slice(PACK * v0, PACK * v1)
-            nc.vector.tensor_tensor(z_woven[:, cols], max012[:, cols], act[3][:, cols], MAX)
             quantize(z_mx, z_woven, v0, v1)
             acc = psum.tile([P, 2, v1 - v0], F32, name="acc")
             for a in range(2):

@@ -24,6 +24,7 @@ def tile_picked_edgecv_gelu_e_kernel(tc, xT, w1, w2, w3, offs, cen, pos1, pos2, 
     nc = tc.nc
     with ExitStack() as ctx:
         keep = ctx.enter_context(tc.tile_pool(name="keep", bufs=1))
+        turns = ctx.enter_context(tc.tile_pool(name="turns", bufs=1))
         psum = ctx.enter_context(tc.psum_pool(name="psum", bufs=8))
 
         def load_list(src, name):
@@ -35,6 +36,9 @@ def tile_picked_edgecv_gelu_e_kernel(tc, xT, w1, w2, w3, offs, cen, pos1, pos2, 
             codes = keep.tile([P, width], U32, name=name + "_codes", tag=name + "_codes", align_bytes=64)
             scales = keep.tile([P, width], U8, name=name + "_scales", align_bytes=64)
             return codes, scales
+
+        def placed(offset, shape, dtype, name):
+            return turns.tile(shape, dtype, name=name, offset=offset, align_bytes=64)
 
         def quantize(mx, woven, c0, c1):
             nc.vector.quantize_mx(
@@ -70,10 +74,6 @@ def tile_picked_edgecv_gelu_e_kernel(tc, xT, w1, w2, w3, offs, cen, pos1, pos2, 
         for b in range(PACK):
             nc.sync.dma_start(w3_raw[b:P:PACK, :, :], w3_rows[b])
 
-        warm = keep.tile([P, 8], F32, name="warm")
-        warm_out = keep.tile([P, 8], F32, name="warm_out")
-        nc.gpsimd.memset(warm[:], 0.0)
-        nc.scalar.activation(warm_out[:], warm[:], GELU)
 
         half = S // 2
         x_woven = [keep.tile([P, half * PACK], BF16, name="x_woven%d" % h, tag="x_woven%d" % h, align_bytes=64) for h in range(2)]
@@ -86,7 +86,10 @@ def tile_picked_edgecv_gelu_e_kernel(tc, xT, w1, w2, w3, offs, cen, pos1, pos2, 
                 nc.scalar.activation(
                     x_slots[h][:, :, j], rounded[:].indirect(offs_sb[:, h * half // 16 : (h + 1) * half // 16]), COPY
                 )
-        pair23 = [keep.tile([P, 2, half], BF16, name="pair23_%d" % h, tag="pair23_%d" % h, align_bytes=64) for h in range(2)]
+        pair23 = [
+            placed(0, [P, 2, half], BF16, "pair23_0"),
+            keep.tile([P, 2, half], BF16, name="pair23_1", tag="pair23_1", align_bytes=64),
+        ]
         for j in range(2):
             for h in range(2):
                 nc.vector.tensor_copy(
@@ -126,41 +129,38 @@ def tile_picked_edgecv_gelu_e_kernel(tc, xT, w1, w2, w3, offs, cen, pos1, pos2, 
         def reuse(tag, shape, dtype, name):
             return keep.tile(shape, dtype, name=name, tag=tag, align_bytes=64)
 
-        centre = [keep.tile([P, V], F32, name="centre%d" % t) for t in range(PACK)]
-        act = [keep.tile([P, D, V], BF16, name="act%d" % t) for t in range(PACK)]
-        pairmax = [keep.tile([P, 2, V], BF16, name="pairmax%d" % t) for t in range(PACK)]
+        act = keep.tile([P, PACK, D, V], BF16, name="act")
+        pairmax = keep.tile([P, PACK, 2, V], BF16, name="pairmax")
         z_early = keep.tile([P, PACK - 1, V], BF16, name="z_early")
         z_woven = keep.tile([P, V * PACK], BF16, name="z_woven", align_bytes=64)
         z_slots = z_woven[:].rearrange("p (v t) -> p v t", t=PACK)
         z_mx = mx_tiles(V, "z")
 
         def fetch_centre(y, t):
-            nc.vector.tensor_copy(centre[t][:], y[:].indirect(cen_sb[:]))
+            nc.vector.tensor_copy(centre[:, t, :], y[:].indirect(cen_sb[:]))
 
         def fetch_edge(dst, e, t, d, v0, v1):
             nc.vector.tensor_tensor(
-                dst[:, v0:v1], e[:].indirect(pos_sb[d][:, v0 // 16 : v1 // 16]), centre[t][:, v0:v1], ADD
+                dst[:, v0:v1], e[:].indirect(pos_sb[d][:, v0 // 16 : v1 // 16]), centre[:, t, v0:v1], ADD
             )
 
-        def largest(t):
-            nc.vector.tensor_tensor(pairmax[t][:], act[t][:, 0:2, :], act[t][:, 2:4, :], MAX)
-            nc.vector.tensor_tensor(z_early[:, t, :], pairmax[t][:, 0, :], pairmax[t][:, 1, :], MAX)
+        def largest_of_pairs(t0, t1):
+            nc.vector.tensor_tensor(pairmax[:, t0:t1], act[:, t0:t1, 0:2, :], act[:, t0:t1, 2:4, :], MAX)
 
         last = PACK - 1
-        tile = reuse("pair23_0", [P, P * PACK], BF16, "w1_woven0")
+        tile = placed(0, [P, P * PACK], BF16, "w1_woven0")
         w1_first = quantize_w(weave_w(nc.scalar.copy, w1_raw, 0, tile[:]), "w1_0")
+        tile = reuse("pair23_1", [P, P * PACK], BF16, "w1_woven1")
+        w1_second = weave_w(nc.scalar.copy, w1_raw, 1, tile[:])
+        tile = placed(0, [P, 2 * P * PACK], BF16, "w1_woven23")
+        weave_w(nc.scalar.copy, w1_raw, 2, tile[:, 0 : P * PACK])
+        weave_w(nc.vector.tensor_copy, w1_raw, 3, tile[:, P * PACK : 2 * P * PACK])
         y0 = keep.tile([P, S], F32, name="y0")
         for h in range(2):
             acc = psum.tile([P, half], F32, name="acc")
             product(acc[:], w1_first, 0, P, x_mx, h * half, (h + 1) * half)
             nc.scalar.copy(y0[:, h * half : (h + 1) * half], acc[:])
-        tile = reuse("pair23_1", [P, P * PACK], BF16, "w1_woven1")
-        y_acc = [None, multiply(quantize_w(weave_w(nc.scalar.copy, w1_raw, 1, tile[:]), "w1_1"))]
-        tile = reuse("pair23_0", [P, 2 * P * PACK], BF16, "w1_woven23")
-        nc.vector.tensor_copy(
-            tile[:].rearrange("p (t q b j) -> p t q j b", t=2, b=PACK, j=PACK),
-            w1_raw[:].rearrange("p j (q t b) -> p t q j b", t=PACK, b=PACK)[:, 2:4],
-        )
+        y_acc = [None, multiply(quantize_w(w1_second, "w1_1"))]
         w1_late = mx_tiles(2 * P, "w1_3")
         quantize(w1_late, tile, 0, 2 * P)
         for t in range(2):
@@ -168,34 +168,37 @@ def tile_picked_edgecv_gelu_e_kernel(tc, xT, w1, w2, w3, offs, cen, pos1, pos2, 
             product(acc[:], w1_late, t * P, (t + 1) * P, x_mx, 0, S)
             y_acc.append(acc)
 
-        def w2_stage(copy, t, tag):
-            tile = reuse(tag, [P, P * PACK], BF16, "w2_woven%d" % t)
-            return weave_w(copy, w2_raw, t, tile[:])
-
-        w2_woven = w2_stage(nc.vector.tensor_copy, 0, "pair23_0")
+        tile = placed(0, [P, P * PACK], BF16, "w2_woven0")
+        e_acc = [multiply(quantize_w(weave_w(nc.vector.tensor_copy, w2_raw, 0, tile[:]), "w2_0"))]
+        centre = placed(0, [P, PACK, V], F32, "centre")
         fetch_centre(y0, 0)
-        e_acc = [multiply(quantize_w(w2_woven, "w2_0"))]
-        fetch_centre(evacuate(y_acc[1], "y1"), 1)
-        fetch_centre(evacuate(y_acc[2], "y2"), 2)
-        fetch_centre(evacuate(y_acc[last], "y3"), last)
-        w2_woven = w2_stage(nc.scalar.copy, 1, "w1_3_codes")
-        e_acc.append(multiply(quantize_w(w2_woven, "w2_1")))
+        for t in range(1, PACK):
+            fetch_centre(evacuate(y_acc[t], "y%d" % t), t)
+        tile = reuse("w1_3_codes", [P, P * PACK], BF16, "w2_woven1")
+        weave_w(nc.scalar.copy, w2_raw, 1, tile[:])
+        w2_second = (placed(4096, [P, P], U32, "w2_1_codes"), keep.tile([P, P], U8, name="w2_1_scales", align_bytes=64))
+        quantize(w2_second, tile, 0, P)
+        e_acc.append(multiply(w2_second))
         e = [evacuate(e_acc[0], "e0")]
-        w2_woven = w2_stage(nc.scalar.copy, 2, "w2_0_codes")
+        tile = placed(4096, [P, 2 * P * PACK], BF16, "w2_woven23")
+        for t in range(2):
+            weave_w(nc.scalar.copy, w2_raw, 2 + t, tile[:, t * P * PACK : (t + 1) * P * PACK])
         edge0 = reuse("edge_even", [P, D, V], F32, "edge0")
         for d in range(D):
             fetch_edge(edge0[:, d, :], e[0], 0, d, 0, V)
-        e_acc.append(multiply(quantize_w(w2_woven, "w2_2")))
+        w2_late = mx_tiles(2 * P, "w2_2")
+        quantize(w2_late, tile, 0, 2 * P)
+        for t in range(2):
+            acc = psum.tile([P, S], F32, name="acc")
+            product(acc[:], w2_late, t * P, (t + 1) * P, x_mx, 0, S)
+            e_acc.append(acc)
         e.append(evacuate(e_acc[1], "e1"))
-        w2_woven = w2_stage(nc.scalar.copy, 3, "w2_1_codes")
-        e_acc.append(multiply(quantize_w(w2_woven, "w2_3")))
-        edge1 = reuse("edge_odd", [P, D, V], F32, "edge1")
+        edge1 = placed(4096, [P, D, V], F32, "edge1")
         for d in range(D):
             fetch_edge(edge1[:, d, :], e[1], 1, d, 0, V)
         e.append(evacuate(e_acc[2], "e2"))
-        nc.scalar.activation(act[0][:], edge0[:], GELU)
+        nc.scalar.activation(act[:, 0], edge0[:], GELU)
         e.append(evacuate(e_acc[3], "e3"))
-        largest(0)
 
         w3_woven = reuse("w2_2_codes", [P, N * PACK], BF16, "w3_woven")
         nc.scalar.copy(
@@ -203,38 +206,47 @@ def tile_picked_edgecv_gelu_e_kernel(tc, xT, w1, w2, w3, offs, cen, pos1, pos2, 
             w3_raw[:].rearrange("p t (c i) -> p c t i", i=4),
         )
         edge2 = reuse("edge_even", [P, D, V], F32, "edge2")
-        nc.scalar.activation(act[1][:], edge1[:], GELU)
+        nc.scalar.activation(act[:, 1], edge1[:], GELU)
         for d in range(D):
             fetch_edge(edge2[:, d, :], e[2], 2, d, 0, V)
             if d % 2 == 1:
-                nc.scalar.activation(act[2][:, d - 1 : d + 1, :], edge2[:, d - 1 : d + 1, :], GELU)
+                nc.scalar.activation(act[:, 2, d - 1 : d + 1, :], edge2[:, d - 1 : d + 1, :], GELU)
         w3_mx = mx_tiles(N, "w3")
         quantize(w3_mx, w3_woven, 0, N)
-        largest(1)
-        edge3a = reuse("edge_odd", [P, V], F32, "edge3a")
+        largest_of_pairs(0, 2)
+        edge3a = placed(4096, [P, V], F32, "edge3a")
         fetch_edge(edge3a[:], e[3], last, 0, 0, V)
-        largest(2)
-        nc.scalar.copy(z_slots[:, :, 0:last], z_early[:].rearrange("p t v -> p v t"))
-        nc.scalar.activation(act[last][:, 0, :], edge3a[:], GELU)
+        largest_of_pairs(2, 3)
+        nc.scalar.activation(act[:, last, 0, :], edge3a[:], GELU)
         edge3b = reuse("edge_even", [P, D - 1, V], F32, "edge3b")
+        nc.vector.tensor_tensor(z_early[:], pairmax[:, 0:last, 0, :], pairmax[:, 0:last, 1, :], MAX)
+        nc.scalar.copy(z_slots[:, :, 0:last], z_early[:].rearrange("p t v -> p v t"))
         for d in (1, 2):
             fetch_edge(edge3b[:, d - 1, :], e[3], last, d, 0, V)
-            nc.scalar.activation(act[last][:, d, :], edge3b[:, d - 1, :], GELU)
+            nc.scalar.activation(act[:, last, d, :], edge3b[:, d - 1, :], GELU)
         chunks = [(0, V // 2), (V // 2, V)]
         for c, (v0, v1) in enumerate(chunks):
             fetch_edge(edge3b[:, 2, :], e[3], last, 3, v0, v1)
-            nc.scalar.activation(act[last][:, 3, v0:v1], edge3b[:, 2, v0:v1], GELU)
+            nc.scalar.activation(act[:, last, 3, v0:v1], edge3b[:, 2, v0:v1], GELU)
             if c == 0:
-                nc.vector.tensor_tensor(pairmax[last][:, 0, :], act[last][:, 0, :], act[last][:, 1, :], MAX)
-        nc.vector.tensor_tensor(pairmax[last][:, 1, :], pairmax[last][:, 0, :], act[last][:, 2, :], MAX)
+                nc.vector.tensor_tensor(pairmax[:, last, 0, :], act[:, last, 0, :], act[:, last, 1, :], MAX)
+        nc.vector.tensor_tensor(pairmax[:, last, 1, :], pairmax[:, last, 0, :], act[:, last, 2, :], MAX)
         out_rows = out.rearrange("(a p) v -> p a v", p=P)
         for v0, v1 in chunks:
-            nc.vector.tensor_tensor(z_slots[:, v0:v1, last], pairmax[last][:, 1, v0:v1], act[last][:, 3, v0:v1], MAX)
+            nc.vector.tensor_tensor(z_slots[:, v0:v1, last], pairmax[:, last, 1, v0:v1], act[:, last, 3, v0:v1], MAX)
         for c, (v0, v1) in enumerate(chunks):
             quantize(z_mx, z_woven, v0, v1)
-            acc = psum.tile([P, 2, v1 - v0], F32, name="acc")
-            for a in range(2):
-                product(acc[:, a, :], w3_mx, a * P, (a + 1) * P, z_mx, v0, v1)
-            result = keep.tile([P, 2, v1 - v0], F32, name="result%d" % c)
-            nc.scalar.copy(result[:], acc[:])
-            nc.sync.dma_start(out_rows[:, :, v0:v1], result[:])
+            if c == 0:
+                acc = psum.tile([P, 2, v1 - v0], F32, name="acc")
+                for a in range(2):
+                    product(acc[:, a, :], w3_mx, a * P, (a + 1) * P, z_mx, v0, v1)
+                result = keep.tile([P, 2, v1 - v0], F32, name="result")
+                nc.scalar.copy(result[:], acc[:])
+                nc.sync.dma_start(out_rows[:, :, v0:v1], result[:])
+            else:
+                for a, (copy, queue) in enumerate(((nc.scalar.copy, nc.scalar), (nc.vector.tensor_copy, nc.sync))):
+                    acc = psum.tile([P, v1 - v0], F32, name="acc")
+                    product(acc[:], w3_mx, a * P, (a + 1) * P, z_mx, v0, v1)
+                    result = keep.tile([P, v1 - v0], F32, name="result_last%d" % a)
+                    copy(result[:], acc[:])
+                    queue.dma_start(out_rows[:, a, v0:v1], result[:])

@@ -75,6 +75,11 @@ def tile_picked_edgecv_gelu_e_kernel(tc, xT, w1, w2, w3, offs, cen, pos1, pos2, 
             nc.sync.dma_start(w3_raw[b:P:PACK, :, :], w3_rows[b])
 
 
+        warm = keep.tile([P, 8], F32, name="warm")
+        warm_out = keep.tile([P, 8], F32, name="warm_out")
+        nc.gpsimd.memset(warm[:], 0.0)
+        nc.scalar.activation(warm_out[:], warm[:], GELU)
+
         half = S // 2
         x_woven = [keep.tile([P, half * PACK], BF16, name="x_woven%d" % h, tag="x_woven%d" % h, align_bytes=64) for h in range(2)]
         x_slots = [tile[:].rearrange("p (n j) -> p n j", j=PACK) for tile in x_woven]
@@ -196,8 +201,8 @@ def tile_picked_edgecv_gelu_e_kernel(tc, xT, w1, w2, w3, offs, cen, pos1, pos2, 
         edge1 = placed(4096, [P, D, V], F32, "edge1")
         for d in range(D):
             fetch_edge(edge1[:, d, :], e[1], 1, d, 0, V)
-        e.append(evacuate(e_acc[2], "e2"))
         nc.scalar.activation(act[:, 0], edge0[:], GELU)
+        e.append(evacuate(e_acc[2], "e2"))
         e.append(evacuate(e_acc[3], "e3"))
 
         w3_woven = reuse("w2_2_codes", [P, N * PACK], BF16, "w3_woven")

@@ -65,9 +65,9 @@ def tile_picked_edgecv_gelu_e_kernel(tc, xT, w1, w2, w3, offs, cen, pos1, pos2, 
             x_plane.append(tile)
         w1_raw = keep.tile([P, PACK, H], F32, name="w1_raw")
         nc.sync.dma_start(w1_raw[:], w1.rearrange("(p j) i -> p j i", j=PACK))
-        cen_sb = load_list(cen, "cen_sb")
         w2_raw = keep.tile([P, PACK, H], F32, name="w2_raw")
         nc.sync.dma_start(w2_raw[:], w2.rearrange("(p j) i -> p j i", j=PACK))
+        cen_sb = load_list(cen, "cen_sb")
         pos_sb = [load_list(src, "pos%d_sb" % d) for d, src in enumerate((pos1, pos2, pos3, pos4))]
         w3_raw = keep.tile([P, PACK, N], F32, name="w3_raw")
         w3_rows = w3.rearrange("(q t b) m -> b q t m", t=PACK, b=PACK)
@@ -100,8 +100,8 @@ def tile_picked_edgecv_gelu_e_kernel(tc, xT, w1, w2, w3, offs, cen, pos1, pos2, 
                 nc.vector.tensor_copy(
                     pair23[h][:, j, :], x_plane[2 + j][:].indirect(offs_sb[:, h * half // 16 : (h + 1) * half // 16])
                 )
-        for h, copy in enumerate((nc.scalar.copy, nc.vector.tensor_copy)):
-            copy(x_slots[h][:, :, 2:4], pair23[h][:].rearrange("p j n -> p n j"))
+        for h in range(2):
+            nc.vector.tensor_copy(x_slots[h][:, :, 2:4], pair23[h][:].rearrange("p j n -> p n j"))
         for h in range(2):
             nc.vector.quantize_mx(
                 out=x_mx[0][:, h * half : (h + 1) * half].bitcast(FP8X4),
@@ -174,7 +174,13 @@ def tile_picked_edgecv_gelu_e_kernel(tc, xT, w1, w2, w3, offs, cen, pos1, pos2, 
             y_acc.append(acc)
 
         tile = placed(0, [P, P * PACK], BF16, "w2_woven0")
-        e_acc = [multiply(quantize_w(weave_w(nc.vector.tensor_copy, w2_raw, 0, tile[:]), "w2_0"))]
+        w2_first = quantize_w(weave_w(nc.vector.tensor_copy, w2_raw, 0, tile[:]), "w2_0")
+        e0_acc = []
+        for h in range(2):
+            acc = psum.tile([P, half], F32, name="acc")
+            product(acc[:], w2_first, 0, P, x_mx, h * half, (h + 1) * half)
+            e0_acc.append(acc)
+        e_acc = [None]
         centre = placed(0, [P, PACK, V], F32, "centre")
         fetch_centre(y0, 0)
         for t in range(1, PACK):
@@ -184,7 +190,9 @@ def tile_picked_edgecv_gelu_e_kernel(tc, xT, w1, w2, w3, offs, cen, pos1, pos2, 
         w2_second = (placed(4096, [P, P], U32, "w2_1_codes"), keep.tile([P, P], U8, name="w2_1_scales", align_bytes=64))
         quantize(w2_second, tile, 0, P)
         e_acc.append(multiply(w2_second))
-        e = [evacuate(e_acc[0], "e0")]
+        e = [keep.tile([P, S], F32, name="e0")]
+        for h in range(2):
+            nc.scalar.copy(e[0][:, h * half : (h + 1) * half], e0_acc[h][:])
         tile = placed(4096, [P, 2 * P * PACK], BF16, "w2_woven23")
         for t in range(2):
             weave_w(nc.scalar.copy, w2_raw, 2 + t, tile[:, t * P * PACK : (t + 1) * P * PACK])

from contextlib import ExitStack

import concourse.mybir as mybir

K, T, S, V, H, N = 512, 1024, 512, 256, 512, 256
D = 4
P = 128
PACK = 4
FLOPS = 2 * (2 * K * H * S + H * N * V)

F32 = mybir.dt.float32
BF16 = mybir.dt.bfloat16
U32 = mybir.dt.uint32
U16 = mybir.dt.uint16
U8 = mybir.dt.uint8
FP8X4 = mybir.dt.float8_e4m3fn_x4
ADD = mybir.AluOpType.add
MAX = mybir.AluOpType.max
COPY = mybir.ActivationFunctionType.Copy
GELU = mybir.ActivationFunctionType.Gelu_apprx_tanh


def tile_picked_edgecv_gelu_e_kernel(tc, xT, w1, w2, w3, offs, cen, pos1, pos2, pos3, pos4, out):
    nc = tc.nc
    with ExitStack() as ctx:
        keep = ctx.enter_context(tc.tile_pool(name="keep", bufs=1))
        turns = ctx.enter_context(tc.tile_pool(name="turns", bufs=1))
        psum = ctx.enter_context(tc.psum_pool(name="psum", bufs=8))

        def load_list(src, name):
            tile = keep.tile([P, src.shape[1]], U16, name=name)
            nc.sync.dma_start(tile[:], src)
            return tile

        def mx_tiles(width, name):
            codes = keep.tile([P, width], U32, name=name + "_codes", tag=name + "_codes", align_bytes=64)
            scales = keep.tile([P, width], U8, name=name + "_scales", align_bytes=64)
            return codes, scales

        def placed(offset, shape, dtype, name):
            return turns.tile(shape, dtype, name=name, offset=offset, align_bytes=64)

        def quantize(mx, woven, c0, c1):
            nc.vector.quantize_mx(
                out=mx[0][:, c0:c1].bitcast(FP8X4), scales=mx[1][:, c0:c1], in_=woven[:, PACK * c0 : PACK * c1]
            )

        def product(acc, lhs, l0, l1, rhs, r0, r1):
            nc.tensor.matmul_mx(
                out=acc,
                lhsT=lhs[0][:, l0:l1].bitcast(FP8X4),
                lhsT_scale=lhs[1][:, l0:l1],
                rhs=rhs[0][:, r0:r1].bitcast(FP8X4),
                rhs_scale=rhs[1][:, r0:r1],
                start=True,
                stop=True,
            )

        offs_sb = load_list(offs, "offs_sb")
        x_rows = xT.rearrange("(p j) t -> j p t", j=PACK)
        x_plane = []
        for j in range(PACK):
            tile = keep.tile([P, T], F32, name="x_plane%d" % j)
            nc.sync.dma_start(tile[:], x_rows[j])
            x_plane.append(tile)
        w1_raw = keep.tile([P, PACK, H], F32, name="w1_raw")
        nc.sync.dma_start(w1_raw[:], w1.rearrange("(p j) i -> p j i", j=PACK))
        w2_raw = keep.tile([P, PACK, H], F32, name="w2_raw")
        nc.sync.dma_start(w2_raw[:], w2.rearrange("(p j) i -> p j i", j=PACK))
        cen_sb = load_list(cen, "cen_sb")
        pos_sb = [load_list(src, "pos%d_sb" % d) for d, src in enumerate((pos1, pos2, pos3, pos4))]
        w3_raw = keep.tile([P, PACK, N], F32, name="w3_raw")
        w3_rows = w3.rearrange("(q t b) m -> b q t m", t=PACK, b=PACK)
        for b in range(PACK):
            nc.sync.dma_start(w3_raw[b:P:PACK, :, :], w3_rows[b])


        warm = keep.tile([P, 8], F32, name="warm")
        warm_out = keep.tile([P, 8], F32, name="warm_out")
        nc.gpsimd.memset(warm[:], 0.0)
        nc.scalar.activation(warm_out[:], warm[:], GELU)

        half = S // 2
        x_woven = [keep.tile([P, half * PACK], BF16, name="x_woven%d" % h, tag="x_woven%d" % h, align_bytes=64) for h in range(2)]
        x_slots = [tile[:].rearrange("p (n j) -> p n j", j=PACK) for tile in x_woven]
        x_mx = mx_tiles(S, "x")
        for j in range(2):
            rounded = keep.tile([P, T], BF16, name="x_rounded%d" % j)
            nc.vector.tensor_copy(rounded[:], x_plane[j][:])
            for h in range(2):
                nc.scalar.activation(
                    x_slots[h][:, :, j], rounded[:].indirect(offs_sb[:, h * half // 16 : (h + 1) * half // 16]), COPY
                )
        pair23 = [
            placed(0, [P, 2, half], BF16, "pair23_0"),
            keep.tile([P, 2, half], BF16, name="pair23_1", tag="pair23_1", align_bytes=64),
        ]
        for j in range(2):
            for h in range(2):
                nc.vector.tensor_copy(
                    pair23[h][:, j, :], x_plane[2 + j][:].indirect(offs_sb[:, h * half // 16 : (h + 1) * half // 16])
                )
        for h in range(2):
            nc.vector.tensor_copy(x_slots[h][:, :, 2:4], pair23[h][:].rearrange("p j n -> p n j"))
        for h in range(2):
            nc.vector.quantize_mx(
                out=x_mx[0][:, h * half : (h + 1) * half].bitcast(FP8X4),
                scales=x_mx[1][:, h * half : (h + 1) * half],
                in_=x_woven[h][:],
            )

        def weave_w(copy, raw, t, woven):
            copy(
                woven.rearrange("p (q b j) -> p q j b", b=PACK, j=PACK),
                raw[:].rearrange("p j (q t b) -> p t q j b", t=PACK, b=PACK)[:, t],
            )
            return woven

        def quantize_w(woven, name):
            mx = mx_tiles(P, name)
            quantize(mx, woven, 0, P)
            return mx

        def multiply(w_mx):
            acc = psum.tile([P, S], F32, name="acc")
            product(acc[:], w_mx, 0, P, x_mx, 0, S)
            return acc

        def evacuate(acc, name):
            rows = keep.tile([P, S], F32, name=name)
            nc.scalar.copy(rows[:], acc[:])
            return rows

        def reuse(tag, shape, dtype, name):
            return keep.tile(shape, dtype, name=name, tag=tag, align_bytes=64)

        act = keep.tile([P, PACK, D, V], BF16, name="act")
        pairmax = keep.tile([P, PACK, 2, V], BF16, name="pairmax")
        z_early = keep.tile([P, PACK - 1, V], BF16, name="z_early")
        z_woven = keep.tile([P, V * PACK], BF16, name="z_woven", align_bytes=64)
        z_slots = z_woven[:].rearrange("p (v t) -> p v t", t=PACK)
        z_mx = mx_tiles(V, "z")

        def fetch_centre(y, t):
            nc.vector.tensor_copy(centre[:, t, :], y[:].indirect(cen_sb[:]))

        def fetch_edge(dst, e, t, d, v0, v1):
            nc.vector.tensor_tensor(
                dst[:, v0:v1], e[:].indirect(pos_sb[d][:, v0 // 16 : v1 // 16]), centre[:, t, v0:v1], ADD
            )

        def largest_of_pairs(t0, t1):
            nc.vector.tensor_tensor(pairmax[:, t0:t1], act[:, t0:t1, 0:2, :], act[:, t0:t1, 2:4, :], MAX)

        last = PACK - 1
        tile = placed(0, [P, P * PACK], BF16, "w1_woven0")
        w1_first = quantize_w(weave_w(nc.scalar.copy, w1_raw, 0, tile[:]), "w1_0")
        tile = reuse("pair23_1", [P, P * PACK], BF16, "w1_woven1")
        w1_second = weave_w(nc.scalar.copy, w1_raw, 1, tile[:])
        tile = placed(0, [P, 2 * P * PACK], BF16, "w1_woven23")
        weave_w(nc.scalar.copy, w1_raw, 2, tile[:, 0 : P * PACK])
        weave_w(nc.vector.tensor_copy, w1_raw, 3, tile[:, P * PACK : 2 * P * PACK])
        y0 = keep.tile([P, S], F32, name="y0")
        for h in range(2):
            acc = psum.tile([P, half], F32, name="acc")
            product(acc[:], w1_first, 0, P, x_mx, h * half, (h + 1) * half)
            nc.scalar.copy(y0[:, h * half : (h + 1) * half], acc[:])
        y_acc = [None, multiply(quantize_w(w1_second, "w1_1"))]
        w1_late = mx_tiles(2 * P, "w1_3")
        quantize(w1_late, tile, 0, 2 * P)
        for t in range(2):
            acc = psum.tile([P, S], F32, name="acc")
            product(acc[:], w1_late, t * P, (t + 1) * P, x_mx, 0, S)
            y_acc.append(acc)

        tile = placed(0, [P, P * PACK], BF16, "w2_woven0")
        w2_first = quantize_w(weave_w(nc.vector.tensor_copy, w2_raw, 0, tile[:]), "w2_0")
        e0_acc = []
        for h in range(2):
            acc = psum.tile([P, half], F32, name="acc")
            product(acc[:], w2_first, 0, P, x_mx, h * half, (h + 1) * half)
            e0_acc.append(acc)
        e_acc = [None]
        centre = placed(0, [P, PACK, V], F32, "centre")
        fetch_centre(y0, 0)
        for t in range(1, PACK):
            fetch_centre(evacuate(y_acc[t], "y%d" % t), t)
        tile = reuse("w1_3_codes", [P, P * PACK], BF16, "w2_woven1")
        weave_w(nc.scalar.copy, w2_raw, 1, tile[:])
        w2_second = (placed(4096, [P, P], U32, "w2_1_codes"), keep.tile([P, P], U8, name="w2_1_scales", align_bytes=64))
        quantize(w2_second, tile, 0, P)
        e_acc.append(multiply(w2_second))
        e = [keep.tile([P, S], F32, name="e0")]
        for h in range(2):
            nc.scalar.copy(e[0][:, h * half : (h + 1) * half], e0_acc[h][:])
        tile = placed(4096, [P, 2 * P * PACK], BF16, "w2_woven23")
        for t in range(2):
            weave_w(nc.scalar.copy, w2_raw, 2 + t, tile[:, t * P * PACK : (t + 1) * P * PACK])
        edge0 = reuse("edge_even", [P, D, V], F32, "edge0")
        for d in range(D):
            fetch_edge(edge0[:, d, :], e[0], 0, d, 0, V)
        w2_late = mx_tiles(2 * P, "w2_2")
        quantize(w2_late, tile, 0, 2 * P)
        for t in range(2):
            acc = psum.tile([P, S], F32, name="acc")
            product(acc[:], w2_late, t * P, (t + 1) * P, x_mx, 0, S)
            e_acc.append(acc)
        e.append(evacuate(e_acc[1], "e1"))
        edge1 = placed(4096, [P, D, V], F32, "edge1")
        for d in range(D):
            fetch_edge(edge1[:, d, :], e[1], 1, d, 0, V)
        nc.scalar.activation(act[:, 0], edge0[:], GELU)
        e.append(evacuate(e_acc[2], "e2"))
        e.append(evacuate(e_acc[3], "e3"))

        w3_woven = reuse("w2_2_codes", [P, N * PACK], BF16, "w3_woven")
        nc.scalar.copy(
            w3_woven[:].rearrange("p (c i t) -> p c t i", i=4, t=PACK),
            w3_raw[:].rearrange("p t (c i) -> p c t i", i=4),
        )
        edge2 = reuse("edge_even", [P, D, V], F32, "edge2")
        nc.scalar.activation(act[:, 1], edge1[:], GELU)
        for d in range(D):
            fetch_edge(edge2[:, d, :], e[2], 2, d, 0, V)
            if d % 2 == 1:
                nc.scalar.activation(act[:, 2, d - 1 : d + 1, :], edge2[:, d - 1 : d + 1, :], GELU)
        w3_mx = mx_tiles(N, "w3")
        quantize(w3_mx, w3_woven, 0, N)
        largest_of_pairs(0, 2)
        edge3a = placed(4096, [P, V], F32, "edge3a")
        fetch_edge(edge3a[:], e[3], last, 0, 0, V)
        largest_of_pairs(2, 3)
        nc.scalar.activation(act[:, last, 0, :], edge3a[:], GELU)
        edge3b = reuse("edge_even", [P, D - 1, V], F32, "edge3b")
        nc.vector.tensor_tensor(z_early[:], pairmax[:, 0:last, 0, :], pairmax[:, 0:last, 1, :], MAX)
        nc.scalar.copy(z_slots[:, :, 0:last], z_early[:].rearrange("p t v -> p v t"))
        for d in (1, 2):
            fetch_edge(edge3b[:, d - 1, :], e[3], last, d, 0, V)
            nc.scalar.activation(act[:, last, d, :], edge3b[:, d - 1, :], GELU)
        chunks = [(0, V // 2), (V // 2, V)]
        for c, (v0, v1) in enumerate(chunks):
            fetch_edge(edge3b[:, 2, :], e[3], last, 3, v0, v1)
            nc.scalar.activation(act[:, last, 3, v0:v1], edge3b[:, 2, v0:v1], GELU)
            if c == 0:
                nc.vector.tensor_tensor(pairmax[:, last, 0, :], act[:, last, 0, :], act[:, last, 1, :], MAX)
        nc.vector.tensor_tensor(pairmax[:, last, 1, :], pairmax[:, last, 0, :], act[:, last, 2, :], MAX)
        out_rows = out.rearrange("(a p) v -> p a v", p=P)
        for v0, v1 in chunks:
            nc.vector.tensor_tensor(z_slots[:, v0:v1, last], pairmax[:, last, 1, v0:v1], act[:, last, 3, v0:v1], MAX)
        for c, (v0, v1) in enumerate(chunks):
            quantize(z_mx, z_woven, v0, v1)
            if c == 0:
                acc = psum.tile([P, 2, v1 - v0], F32, name="acc")
                for a in range(2):
                    product(acc[:, a, :], w3_mx, a * P, (a + 1) * P, z_mx, v0, v1)
                result = keep.tile([P, 2, v1 - v0], F32, name="result")
                nc.scalar.copy(result[:], acc[:])
                nc.sync.dma_start(out_rows[:, :, v0:v1], result[:])
            else:
                for a, (copy, queue) in enumerate(((nc.scalar.copy, nc.scalar), (nc.vector.tensor_copy, nc.sync))):
                    acc = psum.tile([P, v1 - v0], F32, name="acc")
                    product(acc[:], w3_mx, a * P, (a + 1) * P, z_mx, v0, v1)
                    result = keep.tile([P, v1 - v0], F32, name="result_last%d" % a)
                    copy(result[:], acc[:])
                    queue.dma_start(out_rows[:, a, v0:v1], result[:])
